import numpy as np
import ml_dtypes


def mxq(x, axis, fmt="e4m3"):
    dtype, down = {"e4m3": (ml_dtypes.float8_e4m3fn, 7), "e5m2": (ml_dtypes.float8_e5m2, 14)}[fmt]
    v = np.moveaxis(np.asarray(x, np.float32).astype(ml_dtypes.bfloat16).astype(np.float64), axis, -1)
    blocks = v.reshape(v.shape[:-1] + (-1, 32))
    amax = np.abs(blocks).max(-1, keepdims=True)
    byte = np.maximum(np.where(amax > 0, np.frexp(amax)[1] - 1 + 127, 0) - down, 1)
    scale = np.exp2(byte - 127.0)
    codes = (blocks / scale).astype(np.float32).astype(dtype).astype(np.float64)
    return np.moveaxis((codes * scale).reshape(v.shape), -1, axis)


WIDE = False


def mx_kscale(k):
    if not WIDE:
        return np.ones(k)
    levels = np.array([10, -10, 5, -5, 0])
    if k % 512:
        return np.exp2(np.random.permutation(np.resize(levels, k // 32))).repeat(32)
    a = np.empty((k // 512, 16))
    for p in range(k // 512):
        a[p, :8] = np.random.permutation(np.resize(levels, 8))
        for g in range(8):
            far = levels[np.abs(levels - a[p, g]) >= 10]
            a[p, g + 8] = far[np.random.randint(len(far))]
    return np.exp2(a.ravel()).repeat(32)


def f64(x):
    return np.asarray(x).astype(np.float64)


def striped(idx):
    return np.tile(idx.reshape(-1, 16).T, (8, 1)).astype(np.uint16)


def unstriped(offs):
    return offs[:16].T.reshape(-1).astype(np.int64)


def pack_weight(w):
    k, n = w.shape
    w = f64(np.asarray(w, np.float32).astype(ml_dtypes.bfloat16)).reshape(k // 32, 32, n)
    amax = np.abs(w).max(1)
    byte = np.clip(np.where(amax > 0, np.frexp(amax)[1] - 1 + 127 - 7, 1), 1, 254)
    scaled = (w * np.exp2(127.0 - byte)[:, None, :]).reshape(k, n).astype(np.float32)
    words = np.ascontiguousarray(scaled.reshape(k // 512, 128, 4, n).transpose(0, 1, 3, 2)).astype(ml_dtypes.float8_e4m3fn).view(np.uint8)
    return words, np.ascontiguousarray(byte.astype(np.uint8).reshape(k // 512, 16, n))


def unpack_weight(words, scales):
    g, p, n, _ = words.shape
    vals = np.ascontiguousarray(words).view(ml_dtypes.float8_e4m3fn).astype(np.float64) * np.repeat(np.exp2(scales.astype(np.float64) - 127.0), 8, axis=1)[..., None]
    return vals.transpose(0, 1, 3, 2).reshape(g * 512, n)


def relu(v):
    return np.maximum(v, 0.0)


def sigmoid(v):
    return 1.0 / (1.0 + np.exp(-np.maximum(v, -700.0)))


K, T, S, D, N, V = 512, 2048, 1024, 4, 128, 256
P = 2 ** 7


def setup_inputs():
    n = np.random.standard_normal
    s = mx_kscale(K)[:, None]
    packed_xT = pack_weight(n((K, T)) * s)
    return {
        "x_words": packed_xT[0],
        "x_scales": packed_xT[1],
        "w1": (n((K, N)) / np.sqrt(K) / s).astype(np.float32),
        "lam": (np.tile(np.random.uniform(0.5, 1.5, S), (P, 1))).astype(np.float32),
        "one": (np.tile(np.random.uniform(0.8, 1.0, S), (P, 1))).astype(np.float32),
        "base": (n((N, V))).astype(np.float32),
        "offs": striped(np.random.permutation(T)[:S]),
    }


def reference(x_words, x_scales, w1, lam, one, base, offs):
    xq = unpack_weight(x_words, x_scales)[:, unstriped(offs)]
    y = mxq(f64(w1), 0, "e4m3").T @ xq
    pos = relu(y - 0.3)
    pl = pos * f64(lam)[:1]
    psum = pl.reshape(len(pl), -1, D).sum(axis=2)
    ngt = relu(-1.0 * y - 0.3)
    nl = ngt * f64(lam)[:1]
    nsum = nl.reshape(len(nl), -1, D).sum(axis=2)
    sel = sigmoid(6.0 * (psum - nsum))
    kp = np.minimum(4.0 * pos, f64(one)[:1])
    kn = np.minimum(4.0 * ngt, f64(one)[:1])
    return f64(base) + sel * (psum / (kp.reshape(len(kp), -1, D).sum(axis=2) + 0.3)) - ((-1.0 * sel + 1.0) * (nsum / (kn.reshape(len(kn), -1, D).sum(axis=2) + 0.3)))

@@ -1,0 +1,139 @@
+import concourse.mybir as mybir
+from concourse.masks import make_identity
+
+F32 = mybir.dt.float32
+BF16 = mybir.dt.bfloat16
+I32 = mybir.dt.int32
+U32 = mybir.dt.uint32
+U16 = mybir.dt.uint16
+U8 = mybir.dt.uint8
+FP8X4 = mybir.dt.float8_e4m3fn_x4
+ALU = mybir.AluOpType
+ACT = mybir.ActivationFunctionType
+
+P = 128
+T = 2048
+S = 1024
+D = 4
+HALVES = 2
+FLOPS = 2 * 512 * 128 * S
+
+
+def tile_picked_ytiesm_merge_p_kernel(tc, x_words, x_scales, w1, lam, one, base, offs, out):
+    nc = tc.nc
+    with tc.tile_pool(name="sb", bufs=1) as sb, tc.psum_pool(name="ps", bufs=1) as ps:
+        offsets = sb.tile([P, S // 16], U16, name="offsets")
+        nc.sync.dma_start(offsets[:], offs)
+
+        xs = sb.tile([P, T], U8, name="xs", align_bytes=64)
+        nc.vector.memset(xs[:].bitcast(I32), 0)
+        for q in range(4):
+            nc.scalar.dma_start(xs[32 * q : 32 * q + 4, :].bitcast(I32), x_scales[0, 4 * q : 4 * q + 4, :].bitcast(I32))
+
+        w_raw = sb.tile([P, 4, P], F32, name="w_raw")
+        nc.sync.dma_start(w_raw[:], w1.rearrange("(p j) m -> p j m", j=4))
+        xw = sb.tile([P, T], I32, name="xw", align_bytes=64)
+        nc.sync.dma_start(xw[:], x_words[0].rearrange("p n t -> p (n t)").bitcast(I32))
+        lam_t = sb.tile([P, HALVES, 8], F32, name="lam_t")
+        one_t = sb.tile([P, HALVES, 8], F32, name="one_t")
+        nc.sync.dma_start(one_t[:, :, 0:D], one[0].rearrange("(b p d) -> p b d", b=HALVES, d=D))
+        nc.sync.dma_start(lam_t[:, :, 0:D], lam[0].rearrange("(b p d) -> p b d", b=HALVES, d=D))
+        base_t = sb.tile([P, HALVES, P], F32, name="base_t")
+        nc.sync.dma_start(base_t[:], base.rearrange("m (b v) -> m b v", b=HALVES))
+
+        ident = sb.tile([P, P], F32, name="ident")
+        make_identity(nc, ident[:])
+
+        w_bf = sb.tile([P, P, 4], BF16, name="w_bf", align_bytes=64)
+        nc.vector.tensor_copy(w_bf[:], w_raw[:].rearrange("p j m -> p m j"))
+        w_codes = sb.tile([P, P], U32, name="w_codes", align_bytes=64)
+        w_scales = sb.tile([P, P], U8, name="w_scales", align_bytes=64)
+        nc.vector.quantize_mx(out=w_codes[:].bitcast(FP8X4), scales=w_scales[:], in_=w_bf[:].rearrange("p m j -> p (m j)"))
+
+        gs = [sb.tile([P, D, P], U8, name="gs%d" % b, align_bytes=64) for b in range(HALVES)]
+        gw = [sb.tile([P, D, P], U32, name="gw%d" % b, align_bytes=64) for b in range(HALVES)]
+        for b in range(HALVES):
+            nc.vector.tensor_copy(gs[b][:].rearrange("p d v -> p v d"), xs[:].indirect(offsets[:, 32 * b : 32 * b + 32]))
+        for b in range(HALVES):
+            nc.vector.tensor_copy(gw[b][:].rearrange("p d v -> p v d"), xw[:].bitcast(U32).indirect(offsets[:, 32 * b : 32 * b + 32]))
+
+        cut = [[sb.tile([P, 2, 2, P], F32, name="cut%d%d" % (b, h)) for h in range(2)] for b in range(HALVES)]
+        for b in range(HALVES):
+            for h in range(2):
+                y = ps.tile([P, 2, P], F32, name="y%d%d" % (b, h))
+                for e in range(2):
+                    d = 2 * h + e
+                    nc.tensor.matmul_mx(out=y[:, e, :], lhsT=gw[b][:, d, :].bitcast(FP8X4), lhsT_scale=gs[b][:, d, :],
+                                        rhs=w_codes[:].bitcast(FP8X4), rhs_scale=w_scales[:], start=True, stop=True)
+                for sign in range(2):
+                    nc.scalar.activation(cut[b][h][:, sign, :, :], y[:], ACT.Relu, bias=-1.2, scale=4.0 - 8.0 * sign)
+
+        def pair_sum(name, b, h, col, op):
+            first = sb.tile([P, 2, P], F32, name=name + "a%d%d" % (b, h))
+            both = sb.tile([P, 2, P], F32, name=name + "b%d%d" % (b, h))
+            nc.vector.tensor_scalar(first[:], cut[b][h][:, :, 0, :], col[:, b, 2 * h : 2 * h + 1], None, op)
+            nc.vector.scalar_tensor_tensor(both[:], cut[b][h][:, :, 1, :], col[:, b, 2 * h + 1 : 2 * h + 2], first[:], op, ALU.add)
+            return both
+
+        def turn_and_add(bank, parts, slots):
+            for sign in range(2):
+                for i, part in enumerate(parts):
+                    nc.tensor.matmul(bank[:, slots[sign], :], lhsT=part[:, sign, :], rhs=ident[:], is_transpose=True,
+                                     start=(i == 0), stop=(i == len(parts) - 1))
+
+        kb = [ps.tile([P, 2, P], F32, name="kb%d" % b) for b in range(HALVES)]
+        pn = [ps.tile([P, 2, P], F32, name="pn%d" % b) for b in range(HALVES)]
+        dd = [sb.tile([P, 2, P], F32, name="dd%d" % b) for b in range(HALVES)]
+        nsb = [sb.tile([P, P], F32, name="nsb%d" % b) for b in range(HALVES)]
+        den = [sb.tile([P, P], F32, name="den%d" % b) for b in range(HALVES)]
+        uw = [sb.tile([P, 2, P], F32, name="uw%d" % b) for b in range(HALVES)]
+        diff = [sb.tile([P, P], F32, name="diff%d" % b) for b in range(HALVES)]
+        th = [sb.tile([P, P], F32, name="th%d" % b) for b in range(HALVES)]
+        xx = [sb.tile([P, P], F32, name="xx%d" % b) for b in range(HALVES)]
+        yy = [sb.tile([P, P], F32, name="yy%d" % b) for b in range(HALVES)]
+        ss = [sb.tile([P, P], F32, name="ss%d" % b) for b in range(HALVES)]
+        rr = [sb.tile([P, P], F32, name="rr%d" % b) for b in range(HALVES)]
+        rs = [sb.tile([P, P], F32, name="rs%d" % b) for b in range(HALVES)]
+        res = [sb.tile([P, P], F32, name="res%d" % b) for b in range(HALVES)]
+        den2 = sb.tile([P, P], F32, name="den2")
+        inv = sb.tile([P, P], F32, name="inv")
+
+        def counts(b):
+            turn_and_add(kb[b], [pair_sum("k", b, h, one_t, ALU.min) for h in range(2)], (1, 0))
+            nc.scalar.activation(dd[b][:], kb[b][:], ACT.Copy, bias=0.3)
+
+        def vote(b):
+            nc.scalar.copy(nsb[b][:], pn[b][:, 1, :])
+            nc.vector.tensor_tensor(diff[b][:], pn[b][:, 0, :], nsb[b][:], ALU.subtract)
+            nc.scalar.activation(th[b][:], diff[b][:], ACT.Tanh, scale=0.75)
+            nc.vector.tensor_tensor(uw[b][:], pn[b][:], dd[b][:], ALU.mult)
+
+        def blend(b):
+            nc.vector.scalar_tensor_tensor(xx[b][:], th[b][:], 1.0, uw[b][:, 0, :], ALU.add, ALU.mult)
+            nc.vector.scalar_tensor_tensor(yy[b][:], th[b][:], 1.0, uw[b][:, 1, :], ALU.subtract, ALU.mult)
+            nc.vector.tensor_tensor(ss[b][:], xx[b][:], yy[b][:], ALU.add)
+
+        counts(0)
+        turn_and_add(pn[0], [pair_sum("l", 0, h, lam_t, ALU.mult) for h in range(2)], (0, 1))
+        counts(1)
+        nc.vector.tensor_tensor(den[0][:], dd[0][:, 0, :], dd[0][:, 1, :], ALU.mult)
+        vote(0)
+        parts = []
+        for d in range(D):
+            part = sb.tile([P, 2, P], F32, name="ls%d" % d)
+            nc.scalar.activation(part[:], cut[1][d // 2][:, :, d % 2, :], ACT.Copy, scale=lam_t[:, 1, d : d + 1])
+            parts.append(part)
+        turn_and_add(pn[1], parts, (0, 1))
+        nc.vector.tensor_tensor(den[1][:], dd[1][:, 0, :], dd[1][:, 1, :], ALU.mult)
+        blend(0)
+        nc.vector.tensor_tensor(den2[:], den[0][:], den[1][:], ALU.mult)
+        nc.vector.reciprocal(inv[:], den2[:])
+        vote(1)
+        for b in range(HALVES):
+            nc.vector.scalar_tensor_tensor(rr[b][:], inv[:], 0.125, den[1 - b][:], ALU.mult, ALU.mult)
+        blend(1)
+        for b in range(HALVES):
+            nc.vector.tensor_tensor(rs[b][:], ss[b][:], rr[b][:], ALU.mult)
+        for b in range(HALVES):
+            nc.vector.tensor_tensor(res[b][:], rs[b][:], base_t[:, b, :], ALU.add)
+            nc.sync.dma_start(out[:, P * b : P * (b + 1)], res[b][:])

@@ -1,5 +1,4 @@
 import concourse.mybir as mybir
-from concourse.masks import make_identity
 
 F32 = mybir.dt.float32
 BF16 = mybir.dt.bfloat16
@@ -25,24 +24,20 @@ def tile_picked_ytiesm_merge_p_kernel(tc, x_words, x_scales, w1, lam, one, base,
         offsets = sb.tile([P, S // 16], U16, name="offsets")
         nc.sync.dma_start(offsets[:], offs)
 
-        xs = sb.tile([P, T], U8, name="xs", align_bytes=64)
+        xs = sb.tile([P, T], U8, name="xs", tag="scales_then_words", align_bytes=64)
         nc.vector.memset(xs[:].bitcast(I32), 0)
         for q in range(4):
-            nc.scalar.dma_start(xs[32 * q : 32 * q + 4, :].bitcast(I32), x_scales[0, 4 * q : 4 * q + 4, :].bitcast(I32))
+            (nc.sync if q % 2 else nc.scalar).dma_start(xs[32 * q : 32 * q + 4, :].bitcast(I32), x_scales[0, 4 * q : 4 * q + 4, :].bitcast(I32))
 
-        w_raw = sb.tile([P, 4, P], F32, name="w_raw")
+        w_raw = sb.tile([P, 4, P], F32, name="w_raw", tag="w_then_late")
         nc.sync.dma_start(w_raw[:], w1.rearrange("(p j) m -> p j m", j=4))
-        xw = sb.tile([P, T], I32, name="xw", align_bytes=64)
-        nc.sync.dma_start(xw[:], x_words[0].rearrange("p n t -> p (n t)").bitcast(I32))
-        lam_t = sb.tile([P, HALVES, 8], F32, name="lam_t")
-        one_t = sb.tile([P, HALVES, 8], F32, name="one_t")
-        nc.sync.dma_start(one_t[:, :, 0:D], one[0].rearrange("(b p d) -> p b d", b=HALVES, d=D))
-        nc.sync.dma_start(lam_t[:, :, 0:D], lam[0].rearrange("(b p d) -> p b d", b=HALVES, d=D))
-        base_t = sb.tile([P, HALVES, P], F32, name="base_t")
-        nc.sync.dma_start(base_t[:], base.rearrange("m (b v) -> m b v", b=HALVES))
-
+        zeros = sb.tile([P, P], F32, name="zeros", tag="zeros_then_words", align_bytes=64)
         ident = sb.tile([P, P], F32, name="ident")
-        make_identity(nc, ident[:])
+        nc.gpsimd.memset(zeros[:], 0.0)
+        nc.gpsimd.affine_select(out=ident[:], in_=zeros[:], pattern=[[-1, P]], compare_op=ALU.not_equal, fill=1.0,
+                                base=0, channel_multiplier=1)
+        xw = sb.tile([P, T], I32, name="xw", tag="zeros_then_words", align_bytes=64)
+        nc.sync.dma_start(xw[:], x_words[0].rearrange("p n t -> p (n t)").bitcast(I32))
 
         w_bf = sb.tile([P, P, 4], BF16, name="w_bf", align_bytes=64)
         nc.vector.tensor_copy(w_bf[:], w_raw[:].rearrange("p j m -> p m j"))
@@ -50,90 +45,114 @@ def tile_picked_ytiesm_merge_p_kernel(tc, x_words, x_scales, w1, lam, one, base,
         w_scales = sb.tile([P, P], U8, name="w_scales", align_bytes=64)
         nc.vector.quantize_mx(out=w_codes[:].bitcast(FP8X4), scales=w_scales[:], in_=w_bf[:].rearrange("p m j -> p (m j)"))
 
+        base_t = sb.tile([P, HALVES, P], F32, name="base_t", tag="w_then_late")
+        one_t = sb.tile([P, HALVES, 8], F32, name="one_t")
+        lam_t = sb.tile([P, HALVES, 8], F32, name="lam_t")
+        nc.gpsimd.dma_start(one_t[:, :, 0:D], one[0].rearrange("(b p d) -> p b d", b=HALVES, d=D))
+        nc.gpsimd.dma_start(lam_t[:, :, 0:D], lam[0].rearrange("(b p d) -> p b d", b=HALVES, d=D))
+        nc.scalar.dma_start(base_t[:], base.rearrange("m (b v) -> m b v", b=HALVES))
+
         gs = [sb.tile([P, D, P], U8, name="gs%d" % b, align_bytes=64) for b in range(HALVES)]
-        gw = [sb.tile([P, D, P], U32, name="gw%d" % b, align_bytes=64) for b in range(HALVES)]
         for b in range(HALVES):
             nc.vector.tensor_copy(gs[b][:].rearrange("p d v -> p v d"), xs[:].indirect(offsets[:, 32 * b : 32 * b + 32]))
+        gw = sb.tile([P, HALVES * D * P], U32, name="gw", tag="scales_then_words", align_bytes=64)
         for b in range(HALVES):
-            nc.vector.tensor_copy(gw[b][:].rearrange("p d v -> p v d"), xw[:].bitcast(U32).indirect(offsets[:, 32 * b : 32 * b + 32]))
+            nc.vector.tensor_copy(gw[:, 512 * b : 512 * (b + 1)].rearrange("p (d v) -> p v d", d=D),
+                                  xw[:].bitcast(U32).indirect(offsets[:, 32 * b : 32 * b + 32]))
 
         cut = [[sb.tile([P, 2, 2, P], F32, name="cut%d%d" % (b, h)) for h in range(2)] for b in range(HALVES)]
         for b in range(HALVES):
             for h in range(2):
-                y = ps.tile([P, 2, P], F32, name="y%d%d" % (b, h))
+                y = ps.tile([P, 2, P], F32, name="y%d%d" % (b, h), tag="bank%d" % (2 * b + h))
                 for e in range(2):
                     d = 2 * h + e
-                    nc.tensor.matmul_mx(out=y[:, e, :], lhsT=gw[b][:, d, :].bitcast(FP8X4), lhsT_scale=gs[b][:, d, :],
+                    c0 = 512 * b + P * d
+                    nc.tensor.matmul_mx(out=y[:, e, :], lhsT=gw[:, c0 : c0 + P].bitcast(FP8X4), lhsT_scale=gs[b][:, d, :],
                                         rhs=w_codes[:].bitcast(FP8X4), rhs_scale=w_scales[:], start=True, stop=True)
                 for sign in range(2):
                     nc.scalar.activation(cut[b][h][:, sign, :, :], y[:], ACT.Relu, bias=-1.2, scale=4.0 - 8.0 * sign)
 
-        def pair_sum(name, b, h, col, op):
-            first = sb.tile([P, 2, P], F32, name=name + "a%d%d" % (b, h))
-            both = sb.tile([P, 2, P], F32, name=name + "b%d%d" % (b, h))
-            nc.vector.tensor_scalar(first[:], cut[b][h][:, :, 0, :], col[:, b, 2 * h : 2 * h + 1], None, op)
-            nc.vector.scalar_tensor_tensor(both[:], cut[b][h][:, :, 1, :], col[:, b, 2 * h + 1 : 2 * h + 2], first[:], op, ALU.add)
-            return both
 
-        def turn_and_add(bank, parts, slots):
-            for sign in range(2):
-                for i, part in enumerate(parts):
-                    nc.tensor.matmul(bank[:, slots[sign], :], lhsT=part[:, sign, :], rhs=ident[:], is_transpose=True,
-                                     start=(i == 0), stop=(i == len(parts) - 1))
+        def halves(name, shape):
+            return [sb.tile(shape, F32, name=name + "%d" % b) for b in range(HALVES)]
 
-        kb = [ps.tile([P, 2, P], F32, name="kb%d" % b) for b in range(HALVES)]
-        pn = [ps.tile([P, 2, P], F32, name="pn%d" % b) for b in range(HALVES)]
-        dd = [sb.tile([P, 2, P], F32, name="dd%d" % b) for b in range(HALVES)]
-        nsb = [sb.tile([P, P], F32, name="nsb%d" % b) for b in range(HALVES)]
-        den = [sb.tile([P, P], F32, name="den%d" % b) for b in range(HALVES)]
-        uw = [sb.tile([P, 2, P], F32, name="uw%d" % b) for b in range(HALVES)]
-        diff = [sb.tile([P, P], F32, name="diff%d" % b) for b in range(HALVES)]
-        th = [sb.tile([P, P], F32, name="th%d" % b) for b in range(HALVES)]
-        xx = [sb.tile([P, P], F32, name="xx%d" % b) for b in range(HALVES)]
-        yy = [sb.tile([P, P], F32, name="yy%d" % b) for b in range(HALVES)]
-        ss = [sb.tile([P, P], F32, name="ss%d" % b) for b in range(HALVES)]
-        rr = [sb.tile([P, P], F32, name="rr%d" % b) for b in range(HALVES)]
-        rs = [sb.tile([P, P], F32, name="rs%d" % b) for b in range(HALVES)]
-        res = [sb.tile([P, P], F32, name="res%d" % b) for b in range(HALVES)]
-        den2 = sb.tile([P, P], F32, name="den2")
-        inv = sb.tile([P, P], F32, name="inv")
+        def scaled(name, b, d, col, op):
+            part = sb.tile([P, 2, P], F32, name=name + "%d%d" % (b, d))
+            nc.vector.tensor_scalar(part[:], cut[b][d // 2][:, :, d % 2, :], col[:, b, d : d + 1], None, op)
+            return part
 
-        def counts(b):
-            turn_and_add(kb[b], [pair_sum("k", b, h, one_t, ALU.min) for h in range(2)], (1, 0))
-            nc.scalar.activation(dd[b][:], kb[b][:], ACT.Copy, bias=0.3)
+        def scaled_onto(name, b, d, col, op, first):
+            part = sb.tile([P, 2, P], F32, name=name + "%d%d" % (b, d))
+            nc.vector.scalar_tensor_tensor(part[:], cut[b][d // 2][:, :, d % 2, :], col[:, b, d : d + 1], first[:], op, ALU.add)
+            return part
+
+        def weighted_on_scalar(b, d):
+            part = sb.tile([P, 2, P], F32, name="ls%d%d" % (b, d))
+            nc.scalar.activation(part[:], cut[b][d // 2][:, :, d % 2, :], ACT.Copy, scale=lam_t[:, b, d : d + 1])
+            return part
+
+        def turn_and_add(name, bank, parts, sign):
+            target = ps.tile([P, P], F32, name=name, tag="bank%d" % bank)
+            for i, part in enumerate(parts):
+                nc.tensor.matmul(target[:], lhsT=part[:, sign, :], rhs=ident[:], is_transpose=True,
+                                 start=(i == 0), stop=(i == len(parts) - 1))
+            return target
+
+        dn, nsb, den, diff, th, rr = (halves(n, [P, P]) for n in ("dn", "nsb", "den", "diff", "th", "rr"))
+        uu, ww, xx, yy, ss, rs, res = (halves(n, [P, P]) for n in ("uu", "ww", "xx", "yy", "ss", "rs", "res"))
+        den2, inv = halves("den2", [P, P // 2]), halves("inv", [P, P // 2])
+        kp, pp = {}, {}
+
+        def counts(b, parts):
+            kn = turn_and_add("kn%d" % b, 4 - 4 * b, parts, 1)
+            kp[b] = turn_and_add("kp%d" % b, 5 - 4 * b, parts, 0)
+            nc.scalar.activation(dn[b][:], kn[:], ACT.Copy, bias=0.3)
+
+        def sums(b, parts):
+            nn = turn_and_add("nn%d" % b, 6 - 4 * b, parts, 1)
+            pp[b] = turn_and_add("pp%d" % b, 7 - 4 * b, parts, 0)
+            nc.scalar.copy(nsb[b][:], nn[:])
+
+        def invert(b):
+            nc.vector.scalar_tensor_tensor(den[b][:], kp[b][:], 0.3, dn[b][:], ALU.add, ALU.mult)
+            nc.vector.tensor_tensor(den2[b][:], den[b][:, 0 : P // 2], den[b][:, P // 2 : P], ALU.mult)
+            nc.vector.reciprocal(inv[b][:], den2[b][:])
 
         def vote(b):
-            nc.scalar.copy(nsb[b][:], pn[b][:, 1, :])
-            nc.vector.tensor_tensor(diff[b][:], pn[b][:, 0, :], nsb[b][:], ALU.subtract)
+            nc.vector.tensor_tensor(diff[b][:], pp[b][:], nsb[b][:], ALU.subtract)
             nc.scalar.activation(th[b][:], diff[b][:], ACT.Tanh, scale=0.75)
-            nc.vector.tensor_tensor(uw[b][:], pn[b][:], dd[b][:], ALU.mult)
+            nc.vector.tensor_tensor(uu[b][:], pp[b][:], dn[b][:], ALU.mult)
+            nc.vector.scalar_tensor_tensor(ww[b][:], kp[b][:], 0.3, nsb[b][:], ALU.add, ALU.mult)
+
+        def spread(b):
+            nc.vector.scalar_tensor_tensor(rr[b][:].rearrange("p (h v) -> p h v", h=2), inv[b][:].unsqueeze(1).to_broadcast([P, 2, P // 2]), 0.125,
+                                           den[b][:].rearrange("p (h v) -> p h v", h=2)[:, ::-1, :], ALU.mult, ALU.mult)
 
         def blend(b):
-            nc.vector.scalar_tensor_tensor(xx[b][:], th[b][:], 1.0, uw[b][:, 0, :], ALU.add, ALU.mult)
-            nc.vector.scalar_tensor_tensor(yy[b][:], th[b][:], 1.0, uw[b][:, 1, :], ALU.subtract, ALU.mult)
+            nc.vector.scalar_tensor_tensor(xx[b][:], th[b][:], 1.0, uu[b][:], ALU.add, ALU.mult)
+            nc.vector.scalar_tensor_tensor(yy[b][:], th[b][:], 1.0, ww[b][:], ALU.subtract, ALU.mult)
             nc.vector.tensor_tensor(ss[b][:], xx[b][:], yy[b][:], ALU.add)
 
-        counts(0)
-        turn_and_add(pn[0], [pair_sum("l", 0, h, lam_t, ALU.mult) for h in range(2)], (0, 1))
-        counts(1)
-        nc.vector.tensor_tensor(den[0][:], dd[0][:, 0, :], dd[0][:, 1, :], ALU.mult)
-        vote(0)
-        parts = []
-        for d in range(D):
-            part = sb.tile([P, 2, P], F32, name="ls%d" % d)
-            nc.scalar.activation(part[:], cut[1][d // 2][:, :, d % 2, :], ACT.Copy, scale=lam_t[:, 1, d : d + 1])
-            parts.append(part)
-        turn_and_add(pn[1], parts, (0, 1))
-        nc.vector.tensor_tensor(den[1][:], dd[1][:, 0, :], dd[1][:, 1, :], ALU.mult)
-        blend(0)
-        nc.vector.tensor_tensor(den2[:], den[0][:], den[1][:], ALU.mult)
-        nc.vector.reciprocal(inv[:], den2[:])
-        vote(1)
-        for b in range(HALVES):
-            nc.vector.scalar_tensor_tensor(rr[b][:], inv[:], 0.125, den[1 - b][:], ALU.mult, ALU.mult)
-        blend(1)
-        for b in range(HALVES):
+        def finish(b):
             nc.vector.tensor_tensor(rs[b][:], ss[b][:], rr[b][:], ALU.mult)
-        for b in range(HALVES):
             nc.vector.tensor_tensor(res[b][:], rs[b][:], base_t[:, b, :], ALU.add)
             nc.sync.dma_start(out[:, P * b : P * (b + 1)], res[b][:])
+
+        k0 = [scaled("k", 0, d, one_t, ALU.min) for d in range(D)]
+        l0 = [scaled("l", 0, d, lam_t, ALU.mult) for d in range(D)]
+        counts(0, k0)
+        sums(0, l0)
+        k1 = [scaled("k", 1, d, one_t, ALU.min) for d in range(D)]
+        counts(1, k1)
+        invert(0)
+        vote(0)
+        l1 = [weighted_on_scalar(1, d) for d in range(D)]
+        sums(1, l1)
+        invert(1)
+        vote(1)
+        spread(0)
+        blend(0)
+        finish(0)
+        spread(1)
+        blend(1)
+        finish(1)

@@ -20,7 +20,7 @@ FLOPS = 2 * 512 * 128 * S
 
 def tile_picked_ytiesm_merge_p_kernel(tc, x_words, x_scales, w1, lam, one, base, offs, out):
     nc = tc.nc
-    with tc.tile_pool(name="sb", bufs=1) as sb, tc.psum_pool(name="ps", bufs=1) as ps:
+    with tc.tile_pool(name="sb", bufs=1) as sb, tc.tile_pool(name="shared", bufs=1) as shared, tc.psum_pool(name="ps", bufs=1) as ps:
         offsets = sb.tile([P, S // 16], U16, name="offsets")
         nc.sync.dma_start(offsets[:], offs)
 
@@ -29,28 +29,26 @@ def tile_picked_ytiesm_merge_p_kernel(tc, x_words, x_scales, w1, lam, one, base,
         for q in range(4):
             (nc.sync if q % 2 else nc.scalar).dma_start(xs[32 * q : 32 * q + 4, :].bitcast(I32), x_scales[0, 4 * q : 4 * q + 4, :].bitcast(I32))
 
-        w_raw = sb.tile([P, 4, P], F32, name="w_raw", tag="w_then_late")
+        w_raw = sb.tile([P, 4, P], F32, name="w_raw")
         nc.sync.dma_start(w_raw[:], w1.rearrange("(p j) m -> p j m", j=4))
-        zeros = sb.tile([P, P], F32, name="zeros", tag="zeros_then_words", align_bytes=64)
+        zeros = shared.tile([P, P], F32, name="zeros", offset=0)
         ident = sb.tile([P, P], F32, name="ident")
         nc.gpsimd.memset(zeros[:], 0.0)
         nc.gpsimd.affine_select(out=ident[:], in_=zeros[:], pattern=[[-1, P]], compare_op=ALU.not_equal, fill=1.0,
                                 base=0, channel_multiplier=1)
-        xw = sb.tile([P, T], I32, name="xw", tag="zeros_then_words", align_bytes=64)
+        xw = shared.tile([P, T], I32, name="xw", offset=128)
         nc.sync.dma_start(xw[:], x_words[0].rearrange("p n t -> p (n t)").bitcast(I32))
 
         w_bf = sb.tile([P, P, 4], BF16, name="w_bf", align_bytes=64)
-        nc.vector.tensor_copy(w_bf[:], w_raw[:].rearrange("p j m -> p m j"))
+        nc.scalar.copy(w_bf[:], w_raw[:].rearrange("p j m -> p m j"))
         w_codes = sb.tile([P, P], U32, name="w_codes", align_bytes=64)
         w_scales = sb.tile([P, P], U8, name="w_scales", align_bytes=64)
         nc.vector.quantize_mx(out=w_codes[:].bitcast(FP8X4), scales=w_scales[:], in_=w_bf[:].rearrange("p m j -> p (m j)"))
 
-        base_t = sb.tile([P, HALVES, P], F32, name="base_t", tag="w_then_late")
-        one_t = sb.tile([P, HALVES, 8], F32, name="one_t")
-        lam_t = sb.tile([P, HALVES, 8], F32, name="lam_t")
-        nc.gpsimd.dma_start(one_t[:, :, 0:D], one[0].rearrange("(b p d) -> p b d", b=HALVES, d=D))
-        nc.gpsimd.dma_start(lam_t[:, :, 0:D], lam[0].rearrange("(b p d) -> p b d", b=HALVES, d=D))
-        nc.scalar.dma_start(base_t[:], base.rearrange("m (b v) -> m b v", b=HALVES))
+        one_t = shared.tile([P, HALVES, 8], F32, name="one_t", offset=0)
+        lam_t = shared.tile([P, HALVES, 8], F32, name="lam_t", offset=64)
+        nc.sync.dma_start(one_t[:, :, 0:D], one[0].rearrange("(b p d) -> p b d", b=HALVES, d=D))
+        nc.sync.dma_start(lam_t[:, :, 0:D], lam[0].rearrange("(b p d) -> p b d", b=HALVES, d=D))
 
         gs = [sb.tile([P, D, P], U8, name="gs%d" % b, align_bytes=64) for b in range(HALVES)]
         for b in range(HALVES):
@@ -60,18 +58,23 @@ def tile_picked_ytiesm_merge_p_kernel(tc, x_words, x_scales, w1, lam, one, base,
             nc.vector.tensor_copy(gw[:, 512 * b : 512 * (b + 1)].rearrange("p (d v) -> p v d", d=D),
                                   xw[:].bitcast(U32).indirect(offsets[:, 32 * b : 32 * b + 32]))
 
-        cut = [[sb.tile([P, 2, 2, P], F32, name="cut%d%d" % (b, h)) for h in range(2)] for b in range(HALVES)]
-        for b in range(HALVES):
-            for h in range(2):
-                y = ps.tile([P, 2, P], F32, name="y%d%d" % (b, h), tag="bank%d" % (2 * b + h))
-                for e in range(2):
-                    d = 2 * h + e
-                    c0 = 512 * b + P * d
-                    nc.tensor.matmul_mx(out=y[:, e, :], lhsT=gw[:, c0 : c0 + P].bitcast(FP8X4), lhsT_scale=gs[b][:, d, :],
-                                        rhs=w_codes[:].bitcast(FP8X4), rhs_scale=w_scales[:], start=True, stop=True)
-                for sign in range(2):
-                    nc.scalar.activation(cut[b][h][:, sign, :, :], y[:], ACT.Relu, bias=-1.2, scale=4.0 - 8.0 * sign)
+        base_t = shared.tile([P, HALVES, P], F32, name="base_t", offset=128)
+        nc.sync.dma_start(base_t[:], base.rearrange("m (b v) -> m b v", b=HALVES))
 
+        cut = [[sb.tile([P, 2, 2, P], F32, name="cut%d%d" % (b, h)) for h in range(2)] for b in range(HALVES)]
+        y = {}
+
+        def product(b, h):
+            y[b, h] = ps.tile([P, 2, P], F32, name="y%d%d" % (b, h), tag="bank%d" % (2 * b + h))
+            for e in range(2):
+                d = 2 * h + e
+                c0 = 512 * b + P * d
+                nc.tensor.matmul_mx(out=y[b, h][:, e, :], lhsT=gw[:, c0 : c0 + P].bitcast(FP8X4), lhsT_scale=gs[b][:, d, :],
+                                    rhs=w_codes[:].bitcast(FP8X4), rhs_scale=w_scales[:], start=True, stop=True)
+
+        def trim(b, h):
+            for sign in range(2):
+                nc.scalar.activation(cut[b][h][:, sign, :, :], y[b, h][:], ACT.Relu, bias=-1.2, scale=4.0 - 8.0 * sign)
 
         def halves(name, shape):
             return [sb.tile(shape, F32, name=name + "%d" % b) for b in range(HALVES)]
@@ -103,56 +106,58 @@ def tile_picked_ytiesm_merge_p_kernel(tc, x_words, x_scales, w1, lam, one, base,
         den2, inv = halves("den2", [P, P // 2]), halves("inv", [P, P // 2])
         kp, pp = {}, {}
 
+        kn, nn = {}, {}
+        H = P // 2
+        tt, stt = nc.vector.tensor_tensor, nc.vector.scalar_tensor_tensor
+        step = {
+            "dn": lambda b: nc.scalar.activation(dn[b][:], kn[b][:], ACT.Copy, bias=0.3),
+            "nsb": lambda b: nc.scalar.copy(nsb[b][:], nn[b][:]),
+            "den": lambda b: stt(den[b][:], kp[b][:], 0.3, dn[b][:], ALU.add, ALU.mult),
+            "den2": lambda b: tt(den2[b][:], den[b][:, 0:H], den[b][:, H:P], ALU.mult),
+            "inv": lambda b: nc.vector.reciprocal(inv[b][:], den2[b][:]),
+            "diff": lambda b: tt(diff[b][:], pp[b][:], nsb[b][:], ALU.subtract),
+            "th": lambda b: nc.scalar.activation(th[b][:], diff[b][:], ACT.Tanh, scale=0.75),
+            "uu": lambda b: tt(uu[b][:], pp[b][:], dn[b][:], ALU.mult),
+            "ww": lambda b: stt(ww[b][:], kp[b][:], 0.3, nsb[b][:], ALU.add, ALU.mult),
+            "rr": lambda b: stt(rr[b][:].rearrange("p (h v) -> p h v", h=2), inv[b][:].unsqueeze(1).to_broadcast([P, 2, H]), 0.125,
+                                den[b][:].rearrange("p (h v) -> p h v", h=2)[:, ::-1, :], ALU.mult, ALU.mult),
+            "xx": lambda b: stt(xx[b][:], th[b][:], 1.0, uu[b][:], ALU.add, ALU.mult),
+            "yy": lambda b: stt(yy[b][:], th[b][:], 1.0, ww[b][:], ALU.subtract, ALU.mult),
+            "ss": lambda b: tt(ss[b][:], xx[b][:], yy[b][:], ALU.add),
+            "rs": lambda b: tt(rs[b][:], ss[b][:], rr[b][:], ALU.mult),
+            "res": lambda b: tt(res[b][:], rs[b][:], base_t[:, b, :], ALU.add),
+            "out": lambda b: nc.sync.dma_start(out[:, P * b : P * (b + 1)], res[b][:]),
+        }
+
+        def run(names):
+            for n in names.split():
+                step[n[:-1]](int(n[-1]))
+
         def counts(b, parts):
-            kn = turn_and_add("kn%d" % b, 4 - 4 * b, parts, 1)
+            kn[b] = turn_and_add("kn%d" % b, 4 - 4 * b, parts, 1)
             kp[b] = turn_and_add("kp%d" % b, 5 - 4 * b, parts, 0)
-            nc.scalar.activation(dn[b][:], kn[:], ACT.Copy, bias=0.3)
 
         def sums(b, parts):
-            nn = turn_and_add("nn%d" % b, 6 - 4 * b, parts, 1)
+            nn[b] = turn_and_add("nn%d" % b, 6 - 4 * b, parts, 1)
             pp[b] = turn_and_add("pp%d" % b, 7 - 4 * b, parts, 0)
-            nc.scalar.copy(nsb[b][:], nn[:])
 
-        def invert(b):
-            nc.vector.scalar_tensor_tensor(den[b][:], kp[b][:], 0.3, dn[b][:], ALU.add, ALU.mult)
-            nc.vector.tensor_tensor(den2[b][:], den[b][:, 0 : P // 2], den[b][:, P // 2 : P], ALU.mult)
-            nc.vector.reciprocal(inv[b][:], den2[b][:])
-
-        def vote(b):
-            nc.vector.tensor_tensor(diff[b][:], pp[b][:], nsb[b][:], ALU.subtract)
-            nc.scalar.activation(th[b][:], diff[b][:], ACT.Tanh, scale=0.75)
-            nc.vector.tensor_tensor(uu[b][:], pp[b][:], dn[b][:], ALU.mult)
-            nc.vector.scalar_tensor_tensor(ww[b][:], kp[b][:], 0.3, nsb[b][:], ALU.add, ALU.mult)
-
-        def spread(b):
-            nc.vector.scalar_tensor_tensor(rr[b][:].rearrange("p (h v) -> p h v", h=2), inv[b][:].unsqueeze(1).to_broadcast([P, 2, P // 2]), 0.125,
-                                           den[b][:].rearrange("p (h v) -> p h v", h=2)[:, ::-1, :], ALU.mult, ALU.mult)
-
-        def blend(b):
-            nc.vector.scalar_tensor_tensor(xx[b][:], th[b][:], 1.0, uu[b][:], ALU.add, ALU.mult)
-            nc.vector.scalar_tensor_tensor(yy[b][:], th[b][:], 1.0, ww[b][:], ALU.subtract, ALU.mult)
-            nc.vector.tensor_tensor(ss[b][:], xx[b][:], yy[b][:], ALU.add)
-
-        def finish(b):
-            nc.vector.tensor_tensor(rs[b][:], ss[b][:], rr[b][:], ALU.mult)
-            nc.vector.tensor_tensor(res[b][:], rs[b][:], base_t[:, b, :], ALU.add)
-            nc.sync.dma_start(out[:, P * b : P * (b + 1)], res[b][:])
-
+        for b, h in ((0, 0), (0, 1), (1, 0), (1, 1)):
+            product(b, h)
+        trim(0, 0)
+        trim(0, 1)
         k0 = [scaled("k", 0, d, one_t, ALU.min) for d in range(D)]
         l0 = [scaled("l", 0, d, lam_t, ALU.mult) for d in range(D)]
+        trim(1, 0)
         counts(0, k0)
+        run("dn0")
+        trim(1, 1)
         sums(0, l0)
+        run("nsb0")
         k1 = [scaled("k", 1, d, one_t, ALU.min) for d in range(D)]
         counts(1, k1)
-        invert(0)
-        vote(0)
+        run("den0 diff0 th0 den20 uu0 inv0 ww0 dn1")
         l1 = [weighted_on_scalar(1, d) for d in range(D)]
         sums(1, l1)
-        invert(1)
-        vote(1)
-        spread(0)
-        blend(0)
-        finish(0)
-        spread(1)
-        blend(1)
-        finish(1)
+        rs[0] = uu[1]
+        res[0] = ww[1]
+        run("nsb1 xx0 yy0 rr0 den1 ss0 diff1 th1 den21 uu1 ww1 inv1 xx1 yy1 rs0 rr1 ss1 res0 out0 rs1 res1 out1")

@@ -145,8 +145,12 @@ def tile_picked_ytiesm_merge_p_kernel(tc, x_words, x_scales, w1, lam, one, base,
             product(b, h)
         trim(0, 0)
         trim(0, 1)
-        k0 = [scaled("k", 0, d, one_t, ALU.min) for d in range(D)]
-        l0 = [scaled("l", 0, d, lam_t, ALU.mult) for d in range(D)]
+        k0, l0 = [], []
+        for d in (0, 2):
+            k_first = scaled("k", 0, d, one_t, ALU.min)
+            l_first = scaled("l", 0, d, lam_t, ALU.mult)
+            k0.append(scaled_onto("k", 0, d + 1, one_t, ALU.min, k_first))
+            l0.append(scaled_onto("l", 0, d + 1, lam_t, ALU.mult, l_first))
         trim(1, 0)
         counts(0, k0)
         run("dn0")

import concourse.mybir as mybir

F32 = mybir.dt.float32
BF16 = mybir.dt.bfloat16
I32 = mybir.dt.int32
U32 = mybir.dt.uint32
U16 = mybir.dt.uint16
U8 = mybir.dt.uint8
FP8X4 = mybir.dt.float8_e4m3fn_x4
ALU = mybir.AluOpType
ACT = mybir.ActivationFunctionType

P = 128
T = 2048
S = 1024
D = 4
HALVES = 2
FLOPS = 2 * 512 * 128 * S


def tile_picked_ytiesm_merge_p_kernel(tc, x_words, x_scales, w1, lam, one, base, offs, out):
    nc = tc.nc
    with tc.tile_pool(name="sb", bufs=1) as sb, tc.tile_pool(name="shared", bufs=1) as shared, tc.psum_pool(name="ps", bufs=1) as ps:
        offsets = sb.tile([P, S // 16], U16, name="offsets")
        nc.sync.dma_start(offsets[:], offs)

        xs = sb.tile([P, T], U8, name="xs", tag="scales_then_words", align_bytes=64)
        nc.vector.memset(xs[:].bitcast(I32), 0)
        for q in range(4):
            (nc.sync if q % 2 else nc.scalar).dma_start(xs[32 * q : 32 * q + 4, :].bitcast(I32), x_scales[0, 4 * q : 4 * q + 4, :].bitcast(I32))

        w_raw = sb.tile([P, 4, P], F32, name="w_raw")
        nc.sync.dma_start(w_raw[:], w1.rearrange("(p j) m -> p j m", j=4))
        zeros = shared.tile([P, P], F32, name="zeros", offset=0)
        ident = sb.tile([P, P], F32, name="ident")
        nc.gpsimd.memset(zeros[:], 0.0)
        nc.gpsimd.affine_select(out=ident[:], in_=zeros[:], pattern=[[-1, P]], compare_op=ALU.not_equal, fill=1.0,
                                base=0, channel_multiplier=1)
        xw = shared.tile([P, T], I32, name="xw", offset=128)
        nc.sync.dma_start(xw[:], x_words[0].rearrange("p n t -> p (n t)").bitcast(I32))

        w_bf = sb.tile([P, P, 4], BF16, name="w_bf", align_bytes=64)
        nc.scalar.copy(w_bf[:], w_raw[:].rearrange("p j m -> p m j"))
        w_codes = sb.tile([P, P], U32, name="w_codes", align_bytes=64)
        w_scales = sb.tile([P, P], U8, name="w_scales", align_bytes=64)
        nc.vector.quantize_mx(out=w_codes[:].bitcast(FP8X4), scales=w_scales[:], in_=w_bf[:].rearrange("p m j -> p (m j)"))

        one_t = shared.tile([P, HALVES, 8], F32, name="one_t", offset=0)
        lam_t = shared.tile([P, HALVES, 8], F32, name="lam_t", offset=64)
        nc.sync.dma_start(one_t[:, :, 0:D], one[0].rearrange("(b p d) -> p b d", b=HALVES, d=D))
        nc.sync.dma_start(lam_t[:, :, 0:D], lam[0].rearrange("(b p d) -> p b d", b=HALVES, d=D))

        gs = [sb.tile([P, D, P], U8, name="gs%d" % b, align_bytes=64) for b in range(HALVES)]
        for b in range(HALVES):
            nc.vector.tensor_copy(gs[b][:].rearrange("p d v -> p v d"), xs[:].indirect(offsets[:, 32 * b : 32 * b + 32]))
        gw = sb.tile([P, HALVES * D * P], U32, name="gw", tag="scales_then_words", align_bytes=64)
        for b in range(HALVES):
            nc.vector.tensor_copy(gw[:, 512 * b : 512 * (b + 1)].rearrange("p (d v) -> p v d", d=D),
                                  xw[:].bitcast(U32).indirect(offsets[:, 32 * b : 32 * b + 32]))

        base_t = shared.tile([P, HALVES, P], F32, name="base_t", offset=128)
        nc.sync.dma_start(base_t[:], base.rearrange("m (b v) -> m b v", b=HALVES))

        cut = [[sb.tile([P, 2, 2, P], F32, name="cut%d%d" % (b, h)) for h in range(2)] for b in range(HALVES)]
        y = {}

        def product(b, h):
            y[b, h] = ps.tile([P, 2, P], F32, name="y%d%d" % (b, h), tag="bank%d" % (2 * b + h))
            for e in range(2):
                d = 2 * h + e
                c0 = 512 * b + P * d
                nc.tensor.matmul_mx(out=y[b, h][:, e, :], lhsT=gw[:, c0 : c0 + P].bitcast(FP8X4), lhsT_scale=gs[b][:, d, :],
                                    rhs=w_codes[:].bitcast(FP8X4), rhs_scale=w_scales[:], start=True, stop=True)

        def trim(b, h):
            for sign in range(2):
                nc.scalar.activation(cut[b][h][:, sign, :, :], y[b, h][:], ACT.Relu, bias=-1.2, scale=4.0 - 8.0 * sign)

        def halves(name, shape):
            return [sb.tile(shape, F32, name=name + "%d" % b) for b in range(HALVES)]

        def scaled(name, b, d, col, op):
            part = sb.tile([P, 2, P], F32, name=name + "%d%d" % (b, d))
            nc.vector.tensor_scalar(part[:], cut[b][d // 2][:, :, d % 2, :], col[:, b, d : d + 1], None, op)
            return part

        def scaled_onto(name, b, d, col, op, first):
            part = sb.tile([P, 2, P], F32, name=name + "%d%d" % (b, d))
            nc.vector.scalar_tensor_tensor(part[:], cut[b][d // 2][:, :, d % 2, :], col[:, b, d : d + 1], first[:], op, ALU.add)
            return part

        def weighted_on_scalar(b, d):
            part = sb.tile([P, 2, P], F32, name="ls%d%d" % (b, d))
            nc.scalar.activation(part[:], cut[b][d // 2][:, :, d % 2, :], ACT.Copy, scale=lam_t[:, b, d : d + 1])
            return part

        def turn_and_add(name, bank, parts, sign):
            target = ps.tile([P, P], F32, name=name, tag="bank%d" % bank)
            for i, part in enumerate(parts):
                nc.tensor.matmul(target[:], lhsT=part[:, sign, :], rhs=ident[:], is_transpose=True,
                                 start=(i == 0), stop=(i == len(parts) - 1))
            return target

        dn, nsb, den, diff, th, rr = (halves(n, [P, P]) for n in ("dn", "nsb", "den", "diff", "th", "rr"))
        uu, ww, xx, yy, ss, rs, res = (halves(n, [P, P]) for n in ("uu", "ww", "xx", "yy", "ss", "rs", "res"))
        den2, inv = halves("den2", [P, P // 2]), halves("inv", [P, P // 2])
        kp, pp = {}, {}

        kn, nn = {}, {}
        H = P // 2
        tt, stt = nc.vector.tensor_tensor, nc.vector.scalar_tensor_tensor
        step = {
            "dn": lambda b: nc.scalar.activation(dn[b][:], kn[b][:], ACT.Copy, bias=0.3),
            "nsb": lambda b: nc.scalar.copy(nsb[b][:], nn[b][:]),
            "den": lambda b: stt(den[b][:], kp[b][:], 0.3, dn[b][:], ALU.add, ALU.mult),
            "den2": lambda b: tt(den2[b][:], den[b][:, 0:H], den[b][:, H:P], ALU.mult),
            "inv": lambda b: nc.vector.reciprocal(inv[b][:], den2[b][:]),
            "diff": lambda b: tt(diff[b][:], pp[b][:], nsb[b][:], ALU.subtract),
            "th": lambda b: nc.scalar.activation(th[b][:], diff[b][:], ACT.Tanh, scale=0.75),
            "uu": lambda b: tt(uu[b][:], pp[b][:], dn[b][:], ALU.mult),
            "ww": lambda b: stt(ww[b][:], kp[b][:], 0.3, nsb[b][:], ALU.add, ALU.mult),
            "rr": lambda b: stt(rr[b][:].rearrange("p (h v) -> p h v", h=2), inv[b][:].unsqueeze(1).to_broadcast([P, 2, H]), 0.125,
                                den[b][:].rearrange("p (h v) -> p h v", h=2)[:, ::-1, :], ALU.mult, ALU.mult),
            "xx": lambda b: stt(xx[b][:], th[b][:], 1.0, uu[b][:], ALU.add, ALU.mult),
            "yy": lambda b: stt(yy[b][:], th[b][:], 1.0, ww[b][:], ALU.subtract, ALU.mult),
            "ss": lambda b: tt(ss[b][:], xx[b][:], yy[b][:], ALU.add),
            "rs": lambda b: tt(rs[b][:], ss[b][:], rr[b][:], ALU.mult),
            "res": lambda b: tt(res[b][:], rs[b][:], base_t[:, b, :], ALU.add),
            "out": lambda b: nc.sync.dma_start(out[:, P * b : P * (b + 1)], res[b][:]),
        }

        def run(names):
            for n in names.split():
                step[n[:-1]](int(n[-1]))

        def counts(b, parts):
            kn[b] = turn_and_add("kn%d" % b, 4 - 4 * b, parts, 1)
            kp[b] = turn_and_add("kp%d" % b, 5 - 4 * b, parts, 0)

        def sums(b, parts):
            nn[b] = turn_and_add("nn%d" % b, 6 - 4 * b, parts, 1)
            pp[b] = turn_and_add("pp%d" % b, 7 - 4 * b, parts, 0)

        for b, h in ((0, 0), (0, 1), (1, 0), (1, 1)):
            product(b, h)
        trim(0, 0)
        trim(0, 1)
        k0, l0 = [], []
        for d in (0, 2):
            k_first = scaled("k", 0, d, one_t, ALU.min)
            l_first = scaled("l", 0, d, lam_t, ALU.mult)
            k0.append(scaled_onto("k", 0, d + 1, one_t, ALU.min, k_first))
            l0.append(scaled_onto("l", 0, d + 1, lam_t, ALU.mult, l_first))
        trim(1, 0)
        counts(0, k0)
        run("dn0")
        trim(1, 1)
        sums(0, l0)
        run("nsb0")
        k1 = [scaled("k", 1, d, one_t, ALU.min) for d in range(D)]
        counts(1, k1)
        run("den0 diff0 th0 den20 uu0 inv0 ww0 dn1")
        l1 = [weighted_on_scalar(1, d) for d in range(D)]
        sums(1, l1)
        rs[0] = uu[1]
        res[0] = ww[1]
        run("nsb1 xx0 yy0 rr0 den1 ss0 diff1 th1 den21 uu1 ww1 inv1 xx1 yy1 rs0 rr1 ss1 res0 out0 rs1 res1 out1")
